import numpy as np
import ml_dtypes


def mxq(x, axis, fmt="e4m3"):
    dtype, down = {"e4m3": (ml_dtypes.float8_e4m3fn, 7), "e5m2": (ml_dtypes.float8_e5m2, 14)}[fmt]
    v = np.moveaxis(np.asarray(x, np.float32).astype(ml_dtypes.bfloat16).astype(np.float64), axis, -1)
    blocks = v.reshape(v.shape[:-1] + (-1, 32))
    amax = np.abs(blocks).max(-1, keepdims=True)
    byte = np.maximum(np.where(amax > 0, np.frexp(amax)[1] - 1 + 127, 0) - down, 1)
    scale = np.exp2(byte - 127.0)
    codes = (blocks / scale).astype(np.float32).astype(dtype).astype(np.float64)
    return np.moveaxis((codes * scale).reshape(v.shape), -1, axis)


WIDE = False


def mx_kscale(k):
    if not WIDE:
        return np.ones(k)
    levels = np.array([10, -10, 5, -5, 0])
    if k % 512:
        return np.exp2(np.random.permutation(np.resize(levels, k // 32))).repeat(32)
    a = np.empty((k // 512, 16))
    for p in range(k // 512):
        a[p, :8] = np.random.permutation(np.resize(levels, 8))
        for g in range(8):
            far = levels[np.abs(levels - a[p, g]) >= 10]
            a[p, g + 8] = far[np.random.randint(len(far))]
    return np.exp2(a.ravel()).repeat(32)


def f64(x):
    return np.asarray(x).astype(np.float64)


def striped(idx):
    return np.tile(np.asarray(idx).reshape(-1, 16).T, (8, 1)).astype(np.uint16)


def unstriped(offs):
    return offs[:16].T.reshape(-1).astype(np.int64)


E2M1 = np.array([0.0, 0.5, 1.0, 1.5, 2.0, 3.0, 4.0, 6.0, -0.0, -0.5, -1.0, -1.5, -2.0, -3.0, -4.0, -6.0])


def pack_weight(w, fmt):
    k, n = w.shape
    w = f64(np.asarray(w, np.float32).astype(ml_dtypes.bfloat16)).reshape(k // 32, 32, n)
    amax = np.abs(w).max(1)
    if fmt == "e4m3":
        byte = np.frexp(amax)[1] - 1 + 127 - 7
    else:
        mant, ex = np.frexp(amax / 6.0)
        byte = np.where(mant > 0.5, ex, ex - 1) + 127
    byte = np.clip(np.where(amax > 0, byte, 1), 1, 254)
    scaled = (w * np.exp2(127.0 - byte)[:, None, :]).reshape(k, n).astype(np.float32)
    by_word = np.ascontiguousarray(scaled.reshape(k // 512, 128, 4, n).transpose(0, 1, 3, 2))
    if fmt == "e4m3":
        words = by_word.astype(ml_dtypes.float8_e4m3fn).view(np.uint8)
    else:
        c = by_word.astype(ml_dtypes.float4_e2m1fn).view(np.uint8) & 0xF
        words = (c[..., 0::2] | (c[..., 1::2] << 4)).reshape(k // 512, 128, 2 * n)
    return np.ascontiguousarray(words), np.ascontiguousarray(byte.astype(np.uint8).reshape(k // 512, 16, n))


def unpack_weight(words, scales, fmt):
    g, _, n = scales.shape
    words = np.ascontiguousarray(words).reshape(g, 128, n, -1)
    if fmt == "e4m3":
        vals = words.view(ml_dtypes.float8_e4m3fn).astype(np.float64)
    else:
        nib = np.empty((g, 128, n, 4), np.uint8)
        nib[..., 0::2] = words & 0xF
        nib[..., 1::2] = words >> 4
        vals = E2M1[nib]
    vals = vals * np.repeat(np.exp2(scales.astype(np.float64) - 127.0), 8, axis=1)[..., None]
    return vals.transpose(0, 1, 3, 2).reshape(g * 512, n)


D, T, I, Q, G, M = 512, 2048, 512, 128, 64, 512


def setup_inputs():
    n = np.random.standard_normal
    idx = np.random.permutation(T)[:I]
    idx2 = np.random.permutation(T)[:I]
    idx3 = np.random.permutation(M)[:G]
    fd = mx_kscale(D)
    keysp = pack_weight(n((D, T)) / fd[:, None], "e4m3")
    return {
        "query": (n((D, Q)) * 1.0 / np.sqrt(D) * fd[:, None]).astype(np.float32),
        "query2": (n((D, Q)) * 1.0 / np.sqrt(D) * fd[:, None]).astype(np.float32),
        "keys_words": keysp[0],
        "keys_scales": keysp[1],
        "lam": (np.random.uniform(1.0, 3.0, (Q, 1))).astype(np.float32),
        "width": (np.random.uniform(0.3, 0.8, (Q, 1))).astype(np.float32),
        "worth": np.tile(np.random.uniform(0.2, 2.0, T), (128, 1)).astype(np.float32),
        "old": (1.0 * n((Q, M))).astype(np.float32),
        "offs": striped(idx),
        "offs2": striped(idx2),
        "offs3": striped(idx3),
    }


def reference(query, query2, keys_words, keys_scales, lam, width, worth, old, offs, offs2, offs3):
    idx = unstriped(offs)
    idx2 = unstriped(offs2)
    idx3 = unstriped(offs3)
    keysu = unpack_weight(keys_words, keys_scales, "e4m3")
    queryq = mxq(f64(query), 0, "e4m3")
    a = queryq.T @ keysu
    query2q = mxq(f64(query2), 0, "e4m3")
    b = query2q.T @ keysu
    la = np.square(a[:, idx]) + np.square(b[:, idx])
    lb = np.square(a[:, idx2]) + np.square(b[:, idx2])
    s = (a[:, idx] * a[:, idx2] + b[:, idx] * b[:, idx2]) / np.sqrt(la * lb + 0.5) * f64(lam)
    ce = (s - np.mean(s, axis=1, keepdims=True)) / f64(width)
    p = 1.0 / (np.square(ce) + 1.0)
    w = p / np.sum(p, axis=1, keepdims=True)
    ws = w * f64(worth)[:1][:, idx] * 512.0
    wp = ws.reshape(Q, G, I // G).sum(axis=2)
    wf = np.zeros((Q, M))
    wf[:, idx3] = wp
    y = f64(old) + wf
    return y

@@ -1,0 +1,199 @@
+from contextlib import ExitStack
+
+import concourse.mybir as mybir
+
+D, T, I, Q, G, M = 512, 2048, 512, 128, 64, 512
+FLOPS = 2 * 2 * D * Q * T
+
+F32 = mybir.dt.float32
+BF16 = mybir.dt.bfloat16
+I32 = mybir.dt.int32
+U32 = mybir.dt.uint32
+U16 = mybir.dt.uint16
+U8 = mybir.dt.uint8
+FP8X4 = mybir.dt.float8_e4m3fn_x4
+ALU = mybir.AluOpType
+ACT = mybir.ActivationFunctionType
+AX = mybir.AxisListType
+
+P = 128
+PACK = 4
+N = 512
+CHUNKS = T // N
+HALF = I // 2
+RUN = I // G
+KEY_LOADS = [(0, 512), (512, 1024), (1024, 1536), (1536, 1792), (1792, 2048)]
+
+
+def tile_attend_planecos_typical_pagesums_kernel(tc, query, query2, keys_words, keys_scales, lam, width, worth, old, offs, offs2, offs3, out):
+    nc = tc.nc
+    with ExitStack() as ctx:
+        lists = ctx.enter_context(tc.tile_pool(name="lists", bufs=1))
+        keep = ctx.enter_context(tc.tile_pool(name="keep", bufs=1))
+        psum = ctx.enter_context(tc.psum_pool(name="psum", bufs=1))
+
+        key_scales = keep.tile([P, N], U8, name="key_scales", align_bytes=64)
+        warm_in = keep.tile([P, 1], F32, name="warm_in")
+        warm_out = keep.tile([P, 1], F32, name="warm_out")
+        nc.vector.memset(warm_in[:], 1.0)
+
+        raw = [keep.tile([P, PACK, Q], F32, name="raw%d" % j) for j in range(2)]
+        key_words = [keep.tile([P, N], U32, name="key_words%d" % c, align_bytes=64) for c in range(CHUNKS)]
+        words = keys_words[0].rearrange("p n t -> p (n t)")
+
+        def load_query(j, src, queue):
+            queue.dma_start(out=raw[j][:], in_=src.rearrange("(p j) w -> p j w", j=PACK))
+
+        def load_keys(c):
+            lo, hi = KEY_LOADS[c]
+            nc.sync.dma_start(out=key_words[lo // N][:, lo % N : lo % N + hi - lo].bitcast(I32), in_=words[:, lo * PACK : hi * PACK].bitcast(I32))
+
+        load_query(0, query, nc.scalar)
+        for quad in range(4):
+            (nc.sync if quad < 2 else nc.scalar).dma_start(
+                out=key_scales[32 * quad : 32 * quad + 16, :].bitcast(I32),
+                in_=keys_scales[0, 4 * quad : 4 * quad + 4, :].rearrange("r (c n) -> c r n", c=CHUNKS).bitcast(I32),
+            )
+        nc.scalar.activation(out=warm_out[:], in_=warm_in[:], func=ACT.Abs_reciprocal_sqrt)
+        load_keys(0)
+        load_keys(1)
+        load_keys(2)
+        load_query(1, query2, nc.sync)
+        load_keys(3)
+        load_keys(4)
+        idx = lists.tile([P, I // 16], U16, name="idx")
+        idx2 = lists.tile([P, I // 16], U16, name="idx2")
+        idx3 = lists.tile([P, G // 16], U16, name="idx3")
+        nc.sync.dma_start(idx[:], offs)
+        nc.sync.dma_start(idx2[:], offs2)
+        worth_sb = keep.tile([P, T], F32, name="worth_sb")
+        nc.sync.dma_start(out=worth_sb[:], in_=worth)
+        old_sb = keep.tile([P, M], F32, name="old_sb")
+        nc.sync.dma_start(out=old_sb[:], in_=old)
+        nc.sync.dma_start(idx3[:], offs3)
+        lam_sb = keep.tile([P, 1], F32, name="lam_sb")
+        width_sb = keep.tile([P, 1], F32, name="width_sb")
+        nc.gpsimd.dma_start(out=lam_sb[:], in_=lam)
+        nc.gpsimd.dma_start(out=width_sb[:], in_=width)
+
+        placed = keep.tile([P, M], F32, name="placed")
+        nc.vector.memset(placed[:], 0.0)
+
+        codes, scales = [], []
+        for j in range(2):
+            grouped = keep.tile([P, Q, PACK], BF16, name="grouped%d" % j, align_bytes=64)
+            nc.vector.tensor_copy(
+                out=grouped[:].rearrange("p (c i) t -> p c t i", i=4),
+                in_=raw[j][:].rearrange("p t (c i) -> p c t i", i=4),
+            )
+            code = keep.tile([P, Q], U32, name="code%d" % j, align_bytes=64)
+            scale = keep.tile([P, Q], U8, name="scale%d" % j, align_bytes=64)
+            nc.vector.quantize_mx(out=code[:].bitcast(FP8X4), scales=scale[:], in_=grouped[:].rearrange("p w t -> p (w t)"))
+            codes.append(code)
+            scales.append(scale)
+
+        inv_width = keep.tile([P, 1], F32, name="inv_width")
+        factor = keep.tile([P, 1], F32, name="factor")
+        minus_one = keep.tile([P, 1], F32, name="minus_one")
+        nc.gpsimd.memset(minus_one[:], -1.0)
+        nc.gpsimd.tensor_tensor(out=inv_width[:], in0=width_sb[:], in1=minus_one[:], op=ALU.pow)
+        nc.gpsimd.tensor_tensor(out=factor[:], in0=inv_width[:], in1=lam_sb[:], op=ALU.mult)
+
+        a_sb = keep.tile([P, T], F32, name="a_sb")
+        b_sb = keep.tile([P, T], F32, name="b_sb")
+        def product(j, dst, lo, hi, bank_name, copy):
+            plane = lo // N
+            cols = slice(lo - plane * N, hi - plane * N)
+            bank = psum.tile([P, N], F32, name=bank_name)
+            nc.tensor.matmul_mx(
+                out=bank[:, 0 : hi - lo],
+                lhsT=codes[j][:].bitcast(FP8X4),
+                lhsT_scale=scales[j][:],
+                rhs=key_words[plane][:, cols].bitcast(FP8X4),
+                rhs_scale=key_scales[4 * plane : P, cols],
+                start=True,
+                stop=True,
+            )
+            copy(out=dst[:, lo:hi], in_=bank[:, 0 : hi - lo])
+
+        a_copies = [nc.scalar.copy] * 3 + [nc.vector.tensor_copy] * 2
+        for n, (lo, hi) in enumerate(KEY_LOADS):
+            product(0, a_sb, lo, hi, "bank%d" % n, a_copies[n])
+        for c, bank_number in ((3, 5), (0, 3), (1, 4), (2, 5)):
+            product(1, b_sb, c * N, (c + 1) * N, "bank%d" % bank_number, nc.scalar.copy)
+
+        def slots(name, tag=None):
+            return keep.tile([P, I], F32, name=name, tag=tag or name)
+
+        halves = [slice(0, HALF), slice(HALF, I)]
+        a1, a2, b1, b2 = slots("a1"), slots("a2"), slots("b1"), slots("b2")
+        sa1, sa2, sb1, sb2 = slots("sa1"), slots("sa2"), slots("sb1"), slots("sb2")
+        nc.vector.tensor_copy(a1[:], a_sb[:].indirect(idx[:]))
+        nc.vector.tensor_copy(a2[:], a_sb[:].indirect(idx2[:]))
+        nc.vector.tensor_copy(b1[:], b_sb[:].indirect(idx[:]))
+        for h in range(2):
+            nc.vector.tensor_copy(b2[:, halves[h]], b_sb[:].indirect(idx2[:, 16 * h : 16 * (h + 1)]))
+        nc.scalar.activation(out=sa1[:], in_=a1[:], func=ACT.Square)
+        nc.scalar.activation(out=sa2[:], in_=a2[:], func=ACT.Square)
+        nc.scalar.activation(out=sb1[:], in_=b1[:], func=ACT.Square)
+        for h in range(2):
+            nc.scalar.activation(out=sb2[:, halves[h]], in_=b2[:, halves[h]], func=ACT.Square)
+
+        la, lb, ma, lab, dot, score = slots("la"), slots("lb"), slots("ma"), slots("lab"), slots("dot"), slots("score")
+        root = slots("root")
+        mb = sb2
+        nc.vector.tensor_tensor(out=la[:], in0=sa1[:], in1=sb1[:], op=ALU.add)
+        for h in halves:
+            nc.vector.tensor_tensor(out=lb[:, h], in0=sa2[:, h], in1=sb2[:, h], op=ALU.add)
+        for h in halves:
+            nc.vector.tensor_tensor(out=lab[:, h], in0=la[:, h], in1=lb[:, h], op=ALU.mult)
+            nc.scalar.activation(out=root[:, h], in_=lab[:, h], func=ACT.Abs_reciprocal_sqrt, bias=0.5)
+        nc.vector.tensor_tensor(out=ma[:], in0=a1[:], in1=a2[:], op=ALU.mult)
+        for h in halves:
+            nc.vector.tensor_tensor(out=mb[:, h], in0=b1[:, h], in1=b2[:, h], op=ALU.mult)
+        for h in halves:
+            nc.vector.tensor_tensor(out=dot[:, h], in0=ma[:, h], in1=mb[:, h], op=ALU.add)
+        total = keep.tile([P, 1], F32, name="total")
+        nc.vector.scalar_tensor_tensor(
+            out=score[:], in0=dot[:], scalar=factor[:], in1=root[:], op0=ALU.mult, op1=ALU.mult, accum_out=total[:]
+        )
+
+        listed_worth = root
+        nc.vector.tensor_copy(listed_worth[:], worth_sb[:].indirect(idx[:]))
+
+        dev, rootp, part, weighted = slots("dev"), slots("rootp"), slots("part"), slots("weighted")
+        part_sums = [keep.tile([P, 1], F32, name="part_sum%d" % h) for h in range(2)]
+        for h in range(2):
+            nc.scalar.activation(out=dev[:, halves[h]], in_=score[:, halves[h]], func=ACT.Square, scale=-float(I), bias=total[:])
+        for h in range(2):
+            nc.scalar.activation(out=rootp[:, halves[h]], in_=dev[:, halves[h]], func=ACT.Abs_reciprocal_sqrt, scale=1.0 / (I * I), bias=1.0)
+        nc.vector.scalar_tensor_tensor(
+            out=part[:, halves[0]], in0=rootp[:, halves[0]], scalar=1.0, in1=rootp[:, halves[0]], op0=ALU.mult, op1=ALU.mult, accum_out=part_sums[0][:]
+        )
+        nc.scalar.activation(out=part[:, halves[1]], in_=rootp[:, halves[1]], func=ACT.Square, accum_out=part_sums[1][:])
+
+        run_sums = keep.tile([P, G], F32, name="run_sums")
+        mean_part = keep.tile([P, 1], F32, name="mean_part")
+        norm = keep.tile([P, 1], F32, name="norm")
+        for h in range(2):
+            nc.vector.tensor_tensor(out=weighted[:, halves[h]], in0=part[:, halves[h]], in1=listed_worth[:, halves[h]], op=ALU.mult)
+        nc.vector.tensor_scalar(
+            out=mean_part[:], in0=part_sums[0][:], scalar1=part_sums[1][:], scalar2=1.0 / 512.0, op0=ALU.add, op1=ALU.mult
+        )
+        nc.vector.reciprocal(out=norm[:], in_=mean_part[:])
+        for h in range(2):
+            nc.vector.tensor_reduce(
+                out=run_sums[:, h * G // 2 : (h + 1) * G // 2],
+                in_=weighted[:, halves[h]].rearrange("p (g r) -> p g r", r=RUN),
+                axis=AX.X,
+                op=ALU.add,
+            )
+        nc.vector.tensor_copy(placed[:].indirect(idx3[:]), run_sums[:])
+
+        for h, queue in enumerate((nc.sync, nc.scalar)):
+            cols = slice(h * M // 2, (h + 1) * M // 2)
+            result = keep.tile([P, M // 2], F32, name="result%d" % h)
+            nc.vector.scalar_tensor_tensor(
+                out=result[:], in0=placed[:, cols], scalar=norm[:], in1=old_sb[:, cols], op0=ALU.mult, op1=ALU.add
+            )
+            queue.dma_start(out=out[:, cols], in_=result[:])

@@ -48,12 +48,17 @@ def tile_attend_planecos_typical_pagesums_kernel(tc, query, query2, keys_words, 
             lo, hi = KEY_LOADS[c]
             nc.sync.dma_start(out=key_words[lo // N][:, lo % N : lo % N + hi - lo].bitcast(I32), in_=words[:, lo * PACK : hi * PACK].bitcast(I32))
 
-        load_query(0, query, nc.scalar)
-        for quad in range(4):
-            (nc.sync if quad < 2 else nc.scalar).dma_start(
+        def load_scales(quad, queue):
+            queue.dma_start(
                 out=key_scales[32 * quad : 32 * quad + 16, :].bitcast(I32),
                 in_=keys_scales[0, 4 * quad : 4 * quad + 4, :].rearrange("r (c n) -> c r n", c=CHUNKS).bitcast(I32),
             )
+
+        load_scales(0, nc.sync)
+        load_query(0, query, nc.scalar)
+        load_scales(1, nc.sync)
+        load_scales(2, nc.scalar)
+        load_scales(3, nc.scalar)
         nc.scalar.activation(out=warm_out[:], in_=warm_in[:], func=ACT.Abs_reciprocal_sqrt)
         load_keys(0)
         load_keys(1)
@@ -116,7 +121,7 @@ def tile_attend_planecos_typical_pagesums_kernel(tc, query, query2, keys_words, 
             )
             copy(out=dst[:, lo:hi], in_=bank[:, 0 : hi - lo])
 
-        a_copies = [nc.scalar.copy] * 3 + [nc.vector.tensor_copy] * 2
+        a_copies = [nc.scalar.copy] * 4 + [nc.vector.tensor_copy]
         for n, (lo, hi) in enumerate(KEY_LOADS):
             product(0, a_sb, lo, hi, "bank%d" % n, a_copies[n])
         for c, bank_number in ((3, 5), (0, 3), (1, 4), (2, 5)):
@@ -130,27 +135,28 @@ def tile_attend_planecos_typical_pagesums_kernel(tc, query, query2, keys_words, 
         sa1, sa2, sb1, sb2 = slots("sa1"), slots("sa2"), slots("sb1"), slots("sb2")
         nc.vector.tensor_copy(a1[:], a_sb[:].indirect(idx[:]))
         nc.vector.tensor_copy(a2[:], a_sb[:].indirect(idx2[:]))
-        nc.vector.tensor_copy(b1[:], b_sb[:].indirect(idx[:]))
-        for h in range(2):
-            nc.vector.tensor_copy(b2[:, halves[h]], b_sb[:].indirect(idx2[:, 16 * h : 16 * (h + 1)]))
+        for dst, offsets in ((b1, idx), (b2, idx2)):
+            for h in range(2):
+                nc.vector.tensor_copy(dst[:, halves[h]], b_sb[:].indirect(offsets[:, 16 * h : 16 * (h + 1)]))
         nc.scalar.activation(out=sa1[:], in_=a1[:], func=ACT.Square)
         nc.scalar.activation(out=sa2[:], in_=a2[:], func=ACT.Square)
-        nc.scalar.activation(out=sb1[:], in_=b1[:], func=ACT.Square)
-        for h in range(2):
-            nc.scalar.activation(out=sb2[:, halves[h]], in_=b2[:, halves[h]], func=ACT.Square)
+        for dst, src in ((sb1, b1), (sb2, b2)):
+            for h in halves:
+                nc.scalar.activation(out=dst[:, h], in_=src[:, h], func=ACT.Square)
 
-        la, lb, ma, lab, dot, score = slots("la"), slots("lb"), slots("ma"), slots("lab"), slots("dot"), slots("score")
+        la, lb, ma, mb, lab, score = slots("la"), slots("lb"), slots("ma"), slots("mb"), slots("lab"), slots("score")
         root = slots("root")
-        mb = sb2
-        nc.vector.tensor_tensor(out=la[:], in0=sa1[:], in1=sb1[:], op=ALU.add)
+        dot = sb2
+        nc.gpsimd.tensor_tensor(out=ma[:], in0=a1[:], in1=a2[:], op=ALU.mult)
+        for h in halves:
+            nc.gpsimd.tensor_tensor(out=la[:, h], in0=sa1[:, h], in1=sb1[:, h], op=ALU.add)
+        for h in halves:
+            nc.vector.tensor_tensor(out=mb[:, h], in0=b1[:, h], in1=b2[:, h], op=ALU.mult)
         for h in halves:
             nc.vector.tensor_tensor(out=lb[:, h], in0=sa2[:, h], in1=sb2[:, h], op=ALU.add)
         for h in halves:
             nc.vector.tensor_tensor(out=lab[:, h], in0=la[:, h], in1=lb[:, h], op=ALU.mult)
             nc.scalar.activation(out=root[:, h], in_=lab[:, h], func=ACT.Abs_reciprocal_sqrt, bias=0.5)
-        nc.vector.tensor_tensor(out=ma[:], in0=a1[:], in1=a2[:], op=ALU.mult)
-        for h in halves:
-            nc.vector.tensor_tensor(out=mb[:, h], in0=b1[:, h], in1=b2[:, h], op=ALU.mult)
         for h in halves:
             nc.vector.tensor_tensor(out=dot[:, h], in0=ma[:, h], in1=mb[:, h], op=ALU.add)
         total = keep.tile([P, 1], F32, name="total")
@@ -162,32 +168,44 @@ def tile_attend_planecos_typical_pagesums_kernel(tc, query, query2, keys_words, 
         nc.vector.tensor_copy(listed_worth[:], worth_sb[:].indirect(idx[:]))
 
         dev, rootp, part, weighted = slots("dev"), slots("rootp"), slots("part"), slots("weighted")
-        part_sums = [keep.tile([P, 1], F32, name="part_sum%d" % h) for h in range(2)]
-        for h in range(2):
-            nc.scalar.activation(out=dev[:, halves[h]], in_=score[:, halves[h]], func=ACT.Square, scale=-float(I), bias=total[:])
-        for h in range(2):
-            nc.scalar.activation(out=rootp[:, halves[h]], in_=dev[:, halves[h]], func=ACT.Abs_reciprocal_sqrt, scale=1.0 / (I * I), bias=1.0)
+        pieces = [slice(0, 192), slice(192, 384), slice(384, 512)]
+        part_sums = [keep.tile([P, 1], F32, name="part_sum%d" % n) for n in range(3)]
+        for h in pieces:
+            nc.scalar.activation(out=dev[:, h], in_=score[:, h], func=ACT.Square, scale=-float(I), bias=total[:])
+        for h in pieces:
+            nc.scalar.activation(out=rootp[:, h], in_=dev[:, h], func=ACT.Abs_reciprocal_sqrt, scale=1.0 / (I * I), bias=1.0)
         nc.vector.scalar_tensor_tensor(
-            out=part[:, halves[0]], in0=rootp[:, halves[0]], scalar=1.0, in1=rootp[:, halves[0]], op0=ALU.mult, op1=ALU.mult, accum_out=part_sums[0][:]
+            out=part[:, pieces[0]], in0=rootp[:, pieces[0]], scalar=1.0, in1=rootp[:, pieces[0]], op0=ALU.mult, op1=ALU.mult, accum_out=part_sums[0][:]
         )
-        nc.scalar.activation(out=part[:, halves[1]], in_=rootp[:, halves[1]], func=ACT.Square, accum_out=part_sums[1][:])
+        for n in (1, 2):
+            nc.scalar.activation(out=part[:, pieces[n]], in_=rootp[:, pieces[n]], func=ACT.Square, accum_out=part_sums[n][:])
 
         run_sums = keep.tile([P, G], F32, name="run_sums")
-        mean_part = keep.tile([P, 1], F32, name="mean_part")
+        part_total = keep.tile([P, 1], F32, name="part_total")
         norm = keep.tile([P, 1], F32, name="norm")
-        for h in range(2):
-            nc.vector.tensor_tensor(out=weighted[:, halves[h]], in0=part[:, halves[h]], in1=listed_worth[:, halves[h]], op=ALU.mult)
-        nc.vector.tensor_scalar(
-            out=mean_part[:], in0=part_sums[0][:], scalar1=part_sums[1][:], scalar2=1.0 / 512.0, op0=ALU.add, op1=ALU.mult
-        )
-        nc.vector.reciprocal(out=norm[:], in_=mean_part[:])
-        for h in range(2):
+
+        def weigh(h):
+            nc.vector.scalar_tensor_tensor(
+                out=weighted[:, h], in0=part[:, h], scalar=512.0, in1=listed_worth[:, h], op0=ALU.mult, op1=ALU.mult
+            )
+
+        def sum_runs(h):
             nc.vector.tensor_reduce(
-                out=run_sums[:, h * G // 2 : (h + 1) * G // 2],
-                in_=weighted[:, halves[h]].rearrange("p (g r) -> p g r", r=RUN),
+                out=run_sums[:, h.start // RUN : h.stop // RUN],
+                in_=weighted[:, h].rearrange("p (g r) -> p g r", r=RUN),
                 axis=AX.X,
                 op=ALU.add,
             )
+
+        weigh(pieces[0])
+        weigh(pieces[1])
+        weigh(pieces[2])
+        sum_runs(slice(0, pieces[1].stop))
+        nc.vector.tensor_scalar(
+            out=part_total[:], in0=part_sums[0][:], scalar1=part_sums[1][:], scalar2=part_sums[2][:], op0=ALU.add, op1=ALU.add
+        )
+        sum_runs(pieces[2])
+        nc.vector.reciprocal(out=norm[:], in_=part_total[:])
         nc.vector.tensor_copy(placed[:].indirect(idx3[:]), run_sums[:])
 
         for h, queue in enumerate((nc.sync, nc.scalar)):

@@ -54,8 +54,8 @@ def tile_attend_planecos_typical_pagesums_kernel(tc, query, query2, keys_words, 
                 in_=keys_scales[0, 4 * quad : 4 * quad + 4, :].rearrange("r (c n) -> c r n", c=CHUNKS).bitcast(I32),
             )
 
-        load_scales(0, nc.sync)
-        load_query(0, query, nc.scalar)
+        load_scales(0, nc.scalar)
+        load_query(0, query, nc.sync)
         load_scales(1, nc.sync)
         load_scales(2, nc.scalar)
         load_scales(3, nc.scalar)
@@ -133,25 +133,35 @@ def tile_attend_planecos_typical_pagesums_kernel(tc, query, query2, keys_words, 
         halves = [slice(0, HALF), slice(HALF, I)]
         a1, a2, b1, b2 = slots("a1"), slots("a2"), slots("b1"), slots("b2")
         sa1, sa2, sb1, sb2 = slots("sa1"), slots("sa2"), slots("sb1"), slots("sb2")
-        nc.vector.tensor_copy(a1[:], a_sb[:].indirect(idx[:]))
-        nc.vector.tensor_copy(a2[:], a_sb[:].indirect(idx2[:]))
-        for dst, offsets in ((b1, idx), (b2, idx2)):
-            for h in range(2):
-                nc.vector.tensor_copy(dst[:, halves[h]], b_sb[:].indirect(offsets[:, 16 * h : 16 * (h + 1)]))
-        nc.scalar.activation(out=sa1[:], in_=a1[:], func=ACT.Square)
-        nc.scalar.activation(out=sa2[:], in_=a2[:], func=ACT.Square)
-        for dst, src in ((sb1, b1), (sb2, b2)):
-            for h in halves:
-                nc.scalar.activation(out=dst[:, h], in_=src[:, h], func=ACT.Square)
+        def look_up(dst, window, offsets, h):
+            nc.vector.tensor_copy(dst[:, h], window[:].indirect(offsets[:, h.start // 16 : h.stop // 16]))
+
+        def square(dst, src, h):
+            nc.scalar.activation(out=dst[:, h], in_=src[:, h], func=ACT.Square)
+
+        for h in halves:
+            look_up(a1, a_sb, idx, h)
+            look_up(a2, a_sb, idx2, h)
+        for h in halves:
+            look_up(b1, b_sb, idx, h)
+        for h in halves:
+            look_up(b2, b_sb, idx2, h)
+        square(sa1, a1, slice(0, I))
+        for h in halves:
+            square(sa2, a2, h)
+            square(sb1, b1, h)
+        for h in halves:
+            square(sb2, b2, h)
 
         la, lb, ma, mb, lab, score = slots("la"), slots("lb"), slots("ma"), slots("mb"), slots("lab"), slots("score")
         root = slots("root")
         dot = sb2
-        nc.gpsimd.tensor_tensor(out=ma[:], in0=a1[:], in1=a2[:], op=ALU.mult)
         for h in halves:
-            nc.gpsimd.tensor_tensor(out=la[:, h], in0=sa1[:, h], in1=sb1[:, h], op=ALU.add)
+            nc.gpsimd.tensor_tensor(out=ma[:, h], in0=a1[:, h], in1=a2[:, h], op=ALU.mult)
+        nc.gpsimd.tensor_tensor(out=la[:, halves[0]], in0=sa1[:, halves[0]], in1=sb1[:, halves[0]], op=ALU.add)
         for h in halves:
             nc.vector.tensor_tensor(out=mb[:, h], in0=b1[:, h], in1=b2[:, h], op=ALU.mult)
+        nc.vector.tensor_tensor(out=la[:, halves[1]], in0=sa1[:, halves[1]], in1=sb1[:, halves[1]], op=ALU.add)
         for h in halves:
             nc.vector.tensor_tensor(out=lb[:, h], in0=sa2[:, h], in1=sb2[:, h], op=ALU.add)
         for h in halves:

@@ -139,8 +139,8 @@ def tile_attend_planecos_typical_pagesums_kernel(tc, query, query2, keys_words, 
         def square(dst, src, h):
             nc.scalar.activation(out=dst[:, h], in_=src[:, h], func=ACT.Square)
 
+        look_up(a1, a_sb, idx, slice(0, I))
         for h in halves:
-            look_up(a1, a_sb, idx, h)
             look_up(a2, a_sb, idx2, h)
         for h in halves:
             look_up(b1, b_sb, idx, h)
@@ -218,9 +218,8 @@ def tile_attend_planecos_typical_pagesums_kernel(tc, query, query2, keys_words, 
         nc.vector.reciprocal(out=norm[:], in_=part_total[:])
         nc.vector.tensor_copy(placed[:].indirect(idx3[:]), run_sums[:])
 
-        for h, queue in enumerate((nc.sync, nc.scalar)):
-            cols = slice(h * M // 2, (h + 1) * M // 2)
-            result = keep.tile([P, M // 2], F32, name="result%d" % h)
+        for cols, queue in ((slice(0, 192), nc.sync), (slice(192, 384), nc.scalar), (slice(384, M), nc.sync)):
+            result = keep.tile([P, cols.stop - cols.start], F32, name="result%d" % cols.start)
             nc.vector.scalar_tensor_tensor(
                 out=result[:], in0=placed[:, cols], scalar=norm[:], in1=old_sb[:, cols], op0=ALU.mult, op1=ALU.add
             )

from contextlib import ExitStack

import concourse.mybir as mybir

D, T, I, Q, G, M = 512, 2048, 512, 128, 64, 512
FLOPS = 2 * 2 * D * Q * T

F32 = mybir.dt.float32
BF16 = mybir.dt.bfloat16
I32 = mybir.dt.int32
U32 = mybir.dt.uint32
U16 = mybir.dt.uint16
U8 = mybir.dt.uint8
FP8X4 = mybir.dt.float8_e4m3fn_x4
ALU = mybir.AluOpType
ACT = mybir.ActivationFunctionType
AX = mybir.AxisListType

P = 128
PACK = 4
N = 512
CHUNKS = T // N
HALF = I // 2
RUN = I // G
KEY_LOADS = [(0, 512), (512, 1024), (1024, 1536), (1536, 1792), (1792, 2048)]


def tile_attend_planecos_typical_pagesums_kernel(tc, query, query2, keys_words, keys_scales, lam, width, worth, old, offs, offs2, offs3, out):
    nc = tc.nc
    with ExitStack() as ctx:
        lists = ctx.enter_context(tc.tile_pool(name="lists", bufs=1))
        keep = ctx.enter_context(tc.tile_pool(name="keep", bufs=1))
        psum = ctx.enter_context(tc.psum_pool(name="psum", bufs=1))

        key_scales = keep.tile([P, N], U8, name="key_scales", align_bytes=64)
        warm_in = keep.tile([P, 1], F32, name="warm_in")
        warm_out = keep.tile([P, 1], F32, name="warm_out")
        nc.vector.memset(warm_in[:], 1.0)

        raw = [keep.tile([P, PACK, Q], F32, name="raw%d" % j) for j in range(2)]
        key_words = [keep.tile([P, N], U32, name="key_words%d" % c, align_bytes=64) for c in range(CHUNKS)]
        words = keys_words[0].rearrange("p n t -> p (n t)")

        def load_query(j, src, queue):
            queue.dma_start(out=raw[j][:], in_=src.rearrange("(p j) w -> p j w", j=PACK))

        def load_keys(c):
            lo, hi = KEY_LOADS[c]
            nc.sync.dma_start(out=key_words[lo // N][:, lo % N : lo % N + hi - lo].bitcast(I32), in_=words[:, lo * PACK : hi * PACK].bitcast(I32))

        def load_scales(quad, queue):
            queue.dma_start(
                out=key_scales[32 * quad : 32 * quad + 16, :].bitcast(I32),
                in_=keys_scales[0, 4 * quad : 4 * quad + 4, :].rearrange("r (c n) -> c r n", c=CHUNKS).bitcast(I32),
            )

        load_scales(0, nc.scalar)
        load_query(0, query, nc.sync)
        load_scales(1, nc.sync)
        load_scales(2, nc.scalar)
        load_scales(3, nc.scalar)
        nc.scalar.activation(out=warm_out[:], in_=warm_in[:], func=ACT.Abs_reciprocal_sqrt)
        load_keys(0)
        load_keys(1)
        load_keys(2)
        load_query(1, query2, nc.sync)
        load_keys(3)
        load_keys(4)
        idx = lists.tile([P, I // 16], U16, name="idx")
        idx2 = lists.tile([P, I // 16], U16, name="idx2")
        idx3 = lists.tile([P, G // 16], U16, name="idx3")
        nc.sync.dma_start(idx[:], offs)
        nc.sync.dma_start(idx2[:], offs2)
        worth_sb = keep.tile([P, T], F32, name="worth_sb")
        nc.sync.dma_start(out=worth_sb[:], in_=worth)
        old_sb = keep.tile([P, M], F32, name="old_sb")
        nc.sync.dma_start(out=old_sb[:], in_=old)
        nc.sync.dma_start(idx3[:], offs3)
        lam_sb = keep.tile([P, 1], F32, name="lam_sb")
        width_sb = keep.tile([P, 1], F32, name="width_sb")
        nc.gpsimd.dma_start(out=lam_sb[:], in_=lam)
        nc.gpsimd.dma_start(out=width_sb[:], in_=width)

        placed = keep.tile([P, M], F32, name="placed")
        nc.vector.memset(placed[:], 0.0)

        codes, scales = [], []
        for j in range(2):
            grouped = keep.tile([P, Q, PACK], BF16, name="grouped%d" % j, align_bytes=64)
            nc.vector.tensor_copy(
                out=grouped[:].rearrange("p (c i) t -> p c t i", i=4),
                in_=raw[j][:].rearrange("p t (c i) -> p c t i", i=4),
            )
            code = keep.tile([P, Q], U32, name="code%d" % j, align_bytes=64)
            scale = keep.tile([P, Q], U8, name="scale%d" % j, align_bytes=64)
            nc.vector.quantize_mx(out=code[:].bitcast(FP8X4), scales=scale[:], in_=grouped[:].rearrange("p w t -> p (w t)"))
            codes.append(code)
            scales.append(scale)

        inv_width = keep.tile([P, 1], F32, name="inv_width")
        factor = keep.tile([P, 1], F32, name="factor")
        minus_one = keep.tile([P, 1], F32, name="minus_one")
        nc.gpsimd.memset(minus_one[:], -1.0)
        nc.gpsimd.tensor_tensor(out=inv_width[:], in0=width_sb[:], in1=minus_one[:], op=ALU.pow)
        nc.gpsimd.tensor_tensor(out=factor[:], in0=inv_width[:], in1=lam_sb[:], op=ALU.mult)

        a_sb = keep.tile([P, T], F32, name="a_sb")
        b_sb = keep.tile([P, T], F32, name="b_sb")
        def product(j, dst, lo, hi, bank_name, copy):
            plane = lo // N
            cols = slice(lo - plane * N, hi - plane * N)
            bank = psum.tile([P, N], F32, name=bank_name)
            nc.tensor.matmul_mx(
                out=bank[:, 0 : hi - lo],
                lhsT=codes[j][:].bitcast(FP8X4),
                lhsT_scale=scales[j][:],
                rhs=key_words[plane][:, cols].bitcast(FP8X4),
                rhs_scale=key_scales[4 * plane : P, cols],
                start=True,
                stop=True,
            )
            copy(out=dst[:, lo:hi], in_=bank[:, 0 : hi - lo])

        a_copies = [nc.scalar.copy] * 4 + [nc.vector.tensor_copy]
        for n, (lo, hi) in enumerate(KEY_LOADS):
            product(0, a_sb, lo, hi, "bank%d" % n, a_copies[n])
        for c, bank_number in ((3, 5), (0, 3), (1, 4), (2, 5)):
            product(1, b_sb, c * N, (c + 1) * N, "bank%d" % bank_number, nc.scalar.copy)

        def slots(name, tag=None):
            return keep.tile([P, I], F32, name=name, tag=tag or name)

        halves = [slice(0, HALF), slice(HALF, I)]
        a1, a2, b1, b2 = slots("a1"), slots("a2"), slots("b1"), slots("b2")
        sa1, sa2, sb1, sb2 = slots("sa1"), slots("sa2"), slots("sb1"), slots("sb2")
        def look_up(dst, window, offsets, h):
            nc.vector.tensor_copy(dst[:, h], window[:].indirect(offsets[:, h.start // 16 : h.stop // 16]))

        def square(dst, src, h):
            nc.scalar.activation(out=dst[:, h], in_=src[:, h], func=ACT.Square)

        look_up(a1, a_sb, idx, slice(0, I))
        for h in halves:
            look_up(a2, a_sb, idx2, h)
        for h in halves:
            look_up(b1, b_sb, idx, h)
        for h in halves:
            look_up(b2, b_sb, idx2, h)
        square(sa1, a1, slice(0, I))
        for h in halves:
            square(sa2, a2, h)
            square(sb1, b1, h)
        for h in halves:
            square(sb2, b2, h)

        la, lb, ma, mb, lab, score = slots("la"), slots("lb"), slots("ma"), slots("mb"), slots("lab"), slots("score")
        root = slots("root")
        dot = sb2
        for h in halves:
            nc.gpsimd.tensor_tensor(out=ma[:, h], in0=a1[:, h], in1=a2[:, h], op=ALU.mult)
        nc.gpsimd.tensor_tensor(out=la[:, halves[0]], in0=sa1[:, halves[0]], in1=sb1[:, halves[0]], op=ALU.add)
        for h in halves:
            nc.vector.tensor_tensor(out=mb[:, h], in0=b1[:, h], in1=b2[:, h], op=ALU.mult)
        nc.vector.tensor_tensor(out=la[:, halves[1]], in0=sa1[:, halves[1]], in1=sb1[:, halves[1]], op=ALU.add)
        for h in halves:
            nc.vector.tensor_tensor(out=lb[:, h], in0=sa2[:, h], in1=sb2[:, h], op=ALU.add)
        for h in halves:
            nc.vector.tensor_tensor(out=lab[:, h], in0=la[:, h], in1=lb[:, h], op=ALU.mult)
            nc.scalar.activation(out=root[:, h], in_=lab[:, h], func=ACT.Abs_reciprocal_sqrt, bias=0.5)
        for h in halves:
            nc.vector.tensor_tensor(out=dot[:, h], in0=ma[:, h], in1=mb[:, h], op=ALU.add)
        total = keep.tile([P, 1], F32, name="total")
        nc.vector.scalar_tensor_tensor(
            out=score[:], in0=dot[:], scalar=factor[:], in1=root[:], op0=ALU.mult, op1=ALU.mult, accum_out=total[:]
        )

        listed_worth = root
        nc.vector.tensor_copy(listed_worth[:], worth_sb[:].indirect(idx[:]))

        dev, rootp, part, weighted = slots("dev"), slots("rootp"), slots("part"), slots("weighted")
        pieces = [slice(0, 192), slice(192, 384), slice(384, 512)]
        part_sums = [keep.tile([P, 1], F32, name="part_sum%d" % n) for n in range(3)]
        for h in pieces:
            nc.scalar.activation(out=dev[:, h], in_=score[:, h], func=ACT.Square, scale=-float(I), bias=total[:])
        for h in pieces:
            nc.scalar.activation(out=rootp[:, h], in_=dev[:, h], func=ACT.Abs_reciprocal_sqrt, scale=1.0 / (I * I), bias=1.0)
        nc.vector.scalar_tensor_tensor(
            out=part[:, pieces[0]], in0=rootp[:, pieces[0]], scalar=1.0, in1=rootp[:, pieces[0]], op0=ALU.mult, op1=ALU.mult, accum_out=part_sums[0][:]
        )
        for n in (1, 2):
            nc.scalar.activation(out=part[:, pieces[n]], in_=rootp[:, pieces[n]], func=ACT.Square, accum_out=part_sums[n][:])

        run_sums = keep.tile([P, G], F32, name="run_sums")
        part_total = keep.tile([P, 1], F32, name="part_total")
        norm = keep.tile([P, 1], F32, name="norm")

        def weigh(h):
            nc.vector.scalar_tensor_tensor(
                out=weighted[:, h], in0=part[:, h], scalar=512.0, in1=listed_worth[:, h], op0=ALU.mult, op1=ALU.mult
            )

        def sum_runs(h):
            nc.vector.tensor_reduce(
                out=run_sums[:, h.start // RUN : h.stop // RUN],
                in_=weighted[:, h].rearrange("p (g r) -> p g r", r=RUN),
                axis=AX.X,
                op=ALU.add,
            )

        weigh(pieces[0])
        weigh(pieces[1])
        weigh(pieces[2])
        sum_runs(slice(0, pieces[1].stop))
        nc.vector.tensor_scalar(
            out=part_total[:], in0=part_sums[0][:], scalar1=part_sums[1][:], scalar2=part_sums[2][:], op0=ALU.add, op1=ALU.add
        )
        sum_runs(pieces[2])
        nc.vector.reciprocal(out=norm[:], in_=part_total[:])
        nc.vector.tensor_copy(placed[:].indirect(idx3[:]), run_sums[:])

        for cols, queue in ((slice(0, 192), nc.sync), (slice(192, 384), nc.scalar), (slice(384, M), nc.sync)):
            result = keep.tile([P, cols.stop - cols.start], F32, name="result%d" % cols.start)
            nc.vector.scalar_tensor_tensor(
                out=result[:], in0=placed[:, cols], scalar=norm[:], in1=old_sb[:, cols], op0=ALU.mult, op1=ALU.add
            )
            queue.dma_start(out=out[:, cols], in_=result[:])
